import numpy as np
import ml_dtypes


def mxq(x, axis, fmt="e4m3"):
    dtype, down = {"e4m3": (ml_dtypes.float8_e4m3fn, 7), "e5m2": (ml_dtypes.float8_e5m2, 14)}[fmt]
    v = np.moveaxis(np.asarray(x, np.float32).astype(ml_dtypes.bfloat16).astype(np.float64), axis, -1)
    blocks = v.reshape(v.shape[:-1] + (-1, 32))
    amax = np.abs(blocks).max(-1, keepdims=True)
    byte = np.maximum(np.where(amax > 0, np.frexp(amax)[1] - 1 + 127, 0) - down, 1)
    scale = np.exp2(byte - 127.0)
    codes = (blocks / scale).astype(np.float32).astype(dtype).astype(np.float64)
    return np.moveaxis((codes * scale).reshape(v.shape), -1, axis)


WIDE = False


def mx_kscale(k):
    if not WIDE:
        return np.ones(k)
    levels = np.array([10, -10, 5, -5, 0])
    if k % 512:
        return np.exp2(np.random.permutation(np.resize(levels, k // 32))).repeat(32)
    a = np.empty((k // 512, 16))
    for p in range(k // 512):
        a[p, :8] = np.random.permutation(np.resize(levels, 8))
        for g in range(8):
            far = levels[np.abs(levels - a[p, g]) >= 10]
            a[p, g + 8] = far[np.random.randint(len(far))]
    return np.exp2(a.ravel()).repeat(32)


def f64(x):
    return np.asarray(x).astype(np.float64)


def striped(idx):
    return np.tile(idx.reshape(-1, 16).T, (8, 1)).astype(np.uint16)


def unstriped(offs):
    return offs[:16].T.reshape(-1).astype(np.int64)


def striped8(idx):
    return np.concatenate([x.reshape(-1, 16).T for x in idx]).astype(np.uint16)


def runs(offs, k):
    lists = np.stack([offs[16 * r : 16 * r + 16].T.reshape(-1) for r in range(8)]).astype(np.int64)
    return lists[np.arange(k) % 512 // 64]


def pack_weight(w):
    k, n = w.shape
    w = f64(np.asarray(w, np.float32).astype(ml_dtypes.bfloat16)).reshape(k // 32, 32, n)
    amax = np.abs(w).max(1)
    byte = np.clip(np.where(amax > 0, np.frexp(amax)[1] - 1 + 127 - 7, 1), 1, 254)
    scaled = (w * np.exp2(127.0 - byte)[:, None, :]).reshape(k, n).astype(np.float32)
    words = np.ascontiguousarray(scaled.reshape(k // 512, 128, 4, n).transpose(0, 1, 3, 2)).astype(ml_dtypes.float8_e4m3fn).view(np.uint8)
    return words, np.ascontiguousarray(byte.astype(np.uint8).reshape(k // 512, 16, n))


def unpack_weight(words, scales):
    g, p, n, _ = words.shape
    vals = np.ascontiguousarray(words).view(ml_dtypes.float8_e4m3fn).astype(np.float64) * np.repeat(np.exp2(scales.astype(np.float64) - 127.0), 8, axis=1)[..., None]
    return vals.transpose(0, 1, 3, 2).reshape(g * 512, n)


def sigmoid(v):
    return 1.0 / (1.0 + np.exp(-np.maximum(v, -700.0)))

def planes(y):
    n, m = y.shape
    v = y.astype(np.float32).astype(ml_dtypes.bfloat16).astype(np.float64).reshape(n // 32, 32, m)
    top = np.abs(v).max(1)
    byte = np.clip(np.where(top > 0, np.frexp(top)[1] - 1 + 127 - 7, 1), 1, 254)
    codes = (v * np.exp2(127.0 - byte)[:, None, :]).reshape(n, m).astype(np.float32).astype(ml_dtypes.float8_e4m3fn).view(np.uint8)
    words = codes.reshape(n // 512, 128, 4, m).transpose(0, 1, 3, 2)
    return np.ascontiguousarray(words), np.ascontiguousarray(byte.astype(np.uint8).reshape(n // 512, 16, m))


K, T, S, H, C = 512, 2048, 512, 512, 512


def setup_inputs():
    n = np.random.standard_normal
    s = mx_kscale(K)[:, None]
    packed_xT = pack_weight(n((K, T)) * s)
    packed_w1 = pack_weight(n((K, H)) / np.sqrt(K) / s)
    return {
        "x_words": packed_xT[0],
        "x_scales": packed_xT[1],
        "w1_words": packed_w1[0],
        "w1_scales": packed_w1[1],
        "gs": (np.random.uniform(0.5, 1.5, (K, 1)) / s).astype(np.float32),
        "offs": striped(np.random.permutation(T)[:S]),
        "n1": striped8(np.stack([np.random.permutation(S) for _ in range(8)])),
        "n2": striped8(np.stack([np.random.permutation(S) for _ in range(8)])),
        "ca": striped(np.random.permutation(T)[:C]),
        "hc": striped8(np.random.randint(0, T, (8, C))),
        "n3": striped8(np.stack([np.random.permutation(S) for _ in range(8)])),
        "n4": striped8(np.stack([np.random.permutation(S) for _ in range(8)])),
    }


def reference(x_words, x_scales, w1_words, w1_scales, gs, offs, n1, n2, ca, hc, n3, n4):
    x_ca = unpack_weight(x_words, x_scales)[:, unstriped(ca)]
    xq = unpack_weight(x_words, x_scales)[:, unstriped(offs)]
    y = unpack_weight(w1_words, w1_scales).T @ xq
    pa = y[np.arange(H)[:, None], runs(n1, H)]
    pb = y[np.arange(H)[:, None], runs(n2, H)]
    z = f64(gs) * (np.maximum(np.maximum(y, pa), pb) - (0.5 * (np.minimum(np.minimum(y, pa), pb))))
    zq = mxq(z, 0, "e4m3")
    a = 0.0625 * (x_ca.T @ zq)
    x_hc = unpack_weight(x_words, x_scales)[np.arange(K)[:, None], runs(hc, K)]
    b = 0.0625 * (x_hc.T @ zq)
    out_0 = a * (sigmoid(b[np.arange(C)[:, None], runs(n4, C)])) - (0.5 * (a[np.arange(C)[:, None], runs(n3, C)]))
    return (out_0,) + planes(out_0)

@@ -1,0 +1,251 @@
+from contextlib import ExitStack
+
+import concourse.mybir as mybir
+
+K, T, S, H, C = 512, 2048, 512, 512, 512
+FLOPS = 2 * K * H * S + 2 * 2 * K * C * S
+
+F32 = mybir.dt.float32
+BF16 = mybir.dt.bfloat16
+I32 = mybir.dt.int32
+U32 = mybir.dt.uint32
+U16 = mybir.dt.uint16
+U8 = mybir.dt.uint8
+FP8X4 = mybir.dt.float8_e4m3fn_x4
+ACT = mybir.ActivationFunctionType
+ALU = mybir.AluOpType
+
+P = 128
+PACK = 4
+HALF = S // 2
+LIST_COLS = HALF // 16
+
+
+def dealt(ap, run):
+    return ap.rearrange("p (t c i) -> p c t i", t=PACK, i=run)
+
+
+def undealt(ap, run):
+    return ap.rearrange("p (c i t) -> p c t i", t=PACK, i=run)
+
+
+def tile_picked_cdhgatebrange_none_po_kernel(
+    tc, x_words, x_scales, w1_words, w1_scales, gs, offs, n1, n2, ca, hc, n3, n4, out_0, out_1, out_2
+):
+    nc = tc.nc
+    with ExitStack() as ctx:
+        keep = ctx.enter_context(tc.tile_pool(name="keep", bufs=1))
+        shared = ctx.enter_context(tc.tile_pool(name="shared", bufs=1))
+        psum = ctx.enter_context(tc.psum_pool(name="psum", bufs=1))
+
+        def sb(name, shape, dtype):
+            return keep.tile(shape, dtype, name=name, align_bytes=64)
+
+        lists = {}
+
+        def load_list(name, src):
+            lists[name] = sb("list_" + name, [P, S // 16], U16)
+            nc.sync.dma_start(lists[name][:], src)
+
+        def half_list(name, h):
+            return lists[name][:, h * LIST_COLS : (h + 1) * LIST_COLS]
+
+        xw = sb("xw", [P, T], U32)
+        xs = sb("xs", [P, T], U8)
+        w1w = keep.tile([P, H], U32, name="w1w", tag="w1w_then_ca_s", align_bytes=64)
+        w1s = shared.tile([P, H], U8, name="w1s", align_bytes=64, offset=4 * C - H // 2)
+        hc_s = sb("hc_s", [P, C], U8)
+        g = sb("g", [P, PACK], F32)
+
+        xs32 = xs[:].bitcast(I32)
+        w1s32 = w1s[:].bitcast(I32)
+        nc.gpsimd.memset(hc_s[:].bitcast(I32), 0)
+
+        xs_hbm = x_scales[0].bitcast(I32)
+        w1s_hbm = w1_scales[0].bitcast(I32)
+        load_list("offs", offs)
+        for q in range(4):
+            nc.sync.dma_start(xs32[32 * q : 32 * q + 32, :], xs_hbm[4 * q : 4 * q + 4, :].partition_broadcast(8))
+        load_list("hc", hc)
+        nc.sync.dma_start(xw[:].bitcast(I32), x_words[0].rearrange("p n t -> p (n t)").bitcast(I32))
+        nc.sync.dma_start(w1w[:].bitcast(I32), w1_words[0].rearrange("p n t -> p (n t)").bitcast(I32))
+        for q in range(4):
+            nc.sync.dma_start(w1s32[32 * q : 32 * q + 32, :], w1s_hbm[4 * q : 4 * q + 4, :].partition_broadcast(8))
+        load_list("n1", n1)
+        load_list("n2", n2)
+        load_list("ca", ca)
+        nc.sync.dma_start(g[:], gs.rearrange("(p t) o -> p (t o)", t=PACK))
+        load_list("n4", n4)
+        load_list("n3", n3)
+
+        w1w_d = sb("w1w_d", [P, H], U32)
+        w1s_d = sb("w1s_d", [P, H], U8)
+        nc.scalar.copy(dealt(w1w_d[:], 4), undealt(w1w[:], 4))
+
+        xq_w = sb("xq_w", [P, S], U32)
+        xq_s = sb("xq_s", [P, S], U8)
+        hc_sg = sb("hc_sg", [P, C], U8)
+        hc_sd = sb("hc_sd", [P, C], U8)
+        hc_wg = shared.tile([P, C], U32, name="hc_wg", align_bytes=64, offset=0)
+        hc_w = sb("hc_w", [P, C], U32)
+        ca_w = shared.tile([P, C], U32, name="ca_w", align_bytes=64, offset=4 * C)
+        ca_s = keep.tile([P, C], U8, name="ca_s", tag="w1w_then_ca_s", align_bytes=64)
+
+        nc.vector.tensor_copy(xq_s[:], xs[:].indirect(lists["offs"][:]))
+        nc.vector.tensor_copy(hc_sg[:], xs[:].indirect(lists["hc"][:]))
+        nc.vector.tensor_copy(xq_w[:], xw[:].indirect(lists["offs"][:]))
+        nc.vector.tensor_copy(dealt(w1s_d[:], 16), undealt(w1s[:], 16))
+
+        banks = [psum.tile([P, S], F32, name=f"bank{b}") for b in range(8)]
+        y = [sb(f"y{t}", [P, S], F32) for t in range(PACK)]
+        for t in range(PACK):
+            cols = slice(t * P, (t + 1) * P)
+            nc.tensor.matmul_mx(
+                out=banks[t][:],
+                lhsT=w1w_d[:, cols].bitcast(FP8X4),
+                lhsT_scale=w1s_d[:, cols],
+                rhs=xq_w[:].bitcast(FP8X4),
+                rhs_scale=xq_s[:],
+                start=True,
+                stop=True,
+            )
+
+        nc.vector.tensor_copy(dealt(hc_sd[:], 16), undealt(hc_sg[:], 16))
+        hc_sd32 = hc_sd[:].bitcast(I32)
+        hc_s32 = hc_s[:].bitcast(I32)
+        for r in range(4):
+            src = 16 * (r // 2) + r
+            nc.sync.dma_start(hc_s32[r:P:32, :], hc_sd32[src:P:32, :])
+        nc.vector.tensor_copy(hc_wg[:], xw[:].indirect(lists["hc"][:]))
+        nc.vector.tensor_copy(ca_w[:].rearrange("p (t m) -> p m t", t=PACK), xw[:].indirect(lists["ca"][:]))
+        nc.vector.tensor_copy(dealt(hc_w[:], 4), undealt(hc_wg[:], 4))
+        nc.vector.tensor_copy(ca_s[:].rearrange("p (t m) -> p m t", t=PACK), xs[:].indirect(lists["ca"][:]))
+
+        def halves(name, dtype):
+            return [sb(f"{name}{h}", [P, PACK, HALF], dtype) for h in range(2)]
+
+        pa, pb = halves("pa", F32), halves("pb", F32)
+        top2, low2 = halves("top2", F32), halves("low2", F32)
+        top3, low3 = halves("top3", F32), halves("low3", F32)
+        spread = halves("spread", F32)
+        z_rows = sb("z_rows", [P, PACK, HALF], BF16)
+        z_bf = [sb(f"z_bf{h}", [P, HALF * PACK], BF16) for h in range(2)]
+        z_w = [sb(f"z_w{h}", [P, HALF], U32) for h in range(2)]
+        z_s = [sb(f"z_s{h}", [P, HALF], U8) for h in range(2)]
+        na = [sb(f"na{t}", [P, S], F32) for t in range(PACK)]
+        th = [sb(f"th{t}", [P, S], F32) for t in range(PACK)]
+
+        def rows_view(tile):
+            return tile[:].rearrange("p t (c i) -> p c t i", i=4)
+
+        def woven_view(tile):
+            return tile[:].rearrange("p (c i t) -> p c t i", t=PACK, i=4)
+
+        def combine(h, t):
+            nc.vector.scalar_tensor_tensor(
+                spread[h][:, t, :], low3[h][:, t, :], -0.5, top3[h][:, t, :], ALU.mult, ALU.add
+            )
+            if h == 0:
+                nc.scalar.activation(z_rows[:, t, :], spread[h][:, t, :], ACT.Copy, scale=g[:, t : t + 1])
+
+        def weave_z(h):
+            if h == 0:
+                nc.scalar.copy(woven_view(z_bf[h]), rows_view(z_rows))
+            else:
+                g_view = g[:].unsqueeze(1).unsqueeze(3).to_broadcast([P, HALF // 4, PACK, 4])
+                nc.vector.tensor_tensor(woven_view(z_bf[h]), rows_view(spread[h]), g_view, ALU.mult)
+
+        def score_psum(h, t, side):
+            if h == 0:
+                return banks[PACK + t][:, side * HALF : (side + 1) * HALF]
+            return banks[PACK * side + t][:, 0:HALF]
+
+        def score(h):
+            nc.vector.quantize_mx(out=z_w[h][:].bitcast(FP8X4), scales=z_s[h][:], in_=z_bf[h][:])
+            for t in range(PACK):
+                cols = slice(t * P, (t + 1) * P)
+                for side, (words, scales) in enumerate(((hc_w, hc_s), (ca_w, ca_s))):
+                    nc.tensor.matmul_mx(
+                        out=score_psum(h, t, side),
+                        lhsT=words[:, cols].bitcast(FP8X4),
+                        lhsT_scale=scales[:, cols],
+                        rhs=z_w[h][:].bitcast(FP8X4),
+                        rhs_scale=z_s[h][:],
+                        start=True,
+                        stop=True,
+                    )
+
+        def empty_b(h, t):
+            js = slice(h * HALF, (h + 1) * HALF)
+            nc.scalar.activation(th[t][:, js], score_psum(h, t, 0), ACT.Tanh, scale=0.0625 * 0.5)
+
+        def empty_a(h, t):
+            js = slice(h * HALF, (h + 1) * HALF)
+            if h == 0:
+                nc.scalar.activation(na[t][:, js], score_psum(h, t, 1), ACT.Copy, scale=-0.0625 * 0.5)
+            else:
+                nc.vector.tensor_scalar(na[t][:, js], score_psum(h, t, 1), -0.0625 * 0.5, None, ALU.mult)
+
+        units = [(h, t) for h in range(2) for t in range(PACK)]
+        for u, (h, t) in enumerate(units):
+            js = slice(h * HALF, (h + 1) * HALF)
+            if h == 0:
+                nc.scalar.activation(y[t][:], banks[t][:], ACT.Copy)
+            nc.scalar.activation(pa[h][:, t, :], y[t][:].indirect(half_list("n1", h)), ACT.Copy)
+            nc.scalar.activation(pb[h][:, t, :], y[t][:].indirect(half_list("n2", h)), ACT.Copy)
+            nc.vector.tensor_tensor(top2[h][:, t, :], pa[h][:, t, :], pb[h][:, t, :], ALU.max)
+            nc.vector.tensor_tensor(low2[h][:, t, :], pa[h][:, t, :], pb[h][:, t, :], ALU.min)
+            if u > 0:
+                combine(*units[u - 1])
+            nc.vector.tensor_tensor(top3[h][:, t, :], top2[h][:, t, :], y[t][:, js], ALU.max)
+            nc.vector.tensor_tensor(low3[h][:, t, :], low2[h][:, t, :], y[t][:, js], ALU.min)
+            if (h, t) == (1, 2):
+                weave_z(0)
+            if (h, t) == (1, 3):
+                score(0)
+        combine(*units[-1])
+        for t in range(PACK):
+            empty_b(0, t)
+            empty_a(0, t)
+        weave_z(1)
+        score(1)
+        for t in range(PACK):
+            empty_a(1, t)
+
+        gate, gated, res = halves("gate", F32), halves("gated", F32), halves("res", F32)
+        res_bf = [sb(f"res_bf{h}", [P, HALF * PACK], BF16) for h in range(2)]
+        res_w = [sb(f"res_w{h}", [P, HALF], U32) for h in range(2)]
+        res_s = sb("res_s", [P, S], U8)
+        out_rows = out_0.rearrange("(p t) j -> p t j", t=PACK)
+        out_words = out_1[0].rearrange("p n t -> p (n t)").bitcast(I32)
+
+        def finish(h, t):
+            js = slice(h * HALF, (h + 1) * HALF)
+            nc.vector.tensor_tensor(
+                res[h][:, t, :], na[t][:].indirect(half_list("n3", h)), gated[h][:, t, :], ALU.subtract
+            )
+            nc.sync.dma_start(out_rows[:, t, js], res[h][:, t, :])
+
+        def planes(h):
+            js = slice(h * HALF, (h + 1) * HALF)
+            nc.vector.quantize_mx(out=res_w[h][:].bitcast(FP8X4), scales=res_s[:, js], in_=res_bf[h][:])
+            nc.sync.dma_start(out_words[:, js], res_w[h][:].bitcast(I32))
+
+        for u, (h, t) in enumerate(units):
+            js = slice(h * HALF, (h + 1) * HALF)
+            if h == 0:
+                empty_b(1, t)
+            nc.scalar.activation(gate[h][:, t, :], th[t][:].indirect(half_list("n4", h)), ACT.Copy)
+            nc.vector.scalar_tensor_tensor(gated[h][:, t, :], gate[h][:, t, :], 1.0, na[t][:, js], ALU.add, ALU.mult)
+            if u > 0:
+                finish(*units[u - 1])
+        nc.scalar.copy(woven_view(res_bf[0]), rows_view(res[0]))
+        finish(*units[-1])
+        planes(0)
+        nc.vector.tensor_copy(woven_view(res_bf[1]), rows_view(res[1]))
+        planes(1)
+        res_s32 = res_s[:].bitcast(I32)
+        out_scales = out_2[0].bitcast(I32)
+        for q in range(4):
+            queue = nc.sync if q % 2 == 0 else nc.scalar
+            queue.dma_start(out_scales[4 * q : 4 * q + 4, :], res_s32[32 * q : 32 * q + 4, :])

@@ -52,7 +52,7 @@ def tile_picked_cdhgatebrange_none_po_kernel(
 
         xw = sb("xw", [P, T], U32)
         xs = sb("xs", [P, T], U8)
-        w1w = keep.tile([P, H], U32, name="w1w", tag="w1w_then_ca_s", align_bytes=64)
+        w1w = shared.tile([P, H], U32, name="w1w", align_bytes=64, offset=8 * C)
         w1s = shared.tile([P, H], U8, name="w1s", align_bytes=64, offset=4 * C - H // 2)
         hc_s = sb("hc_s", [P, C], U8)
         g = sb("g", [P, PACK], F32)
@@ -84,15 +84,20 @@ def tile_picked_cdhgatebrange_none_po_kernel(
 
         xq_w = sb("xq_w", [P, S], U32)
         xq_s = sb("xq_s", [P, S], U8)
-        hc_sg = sb("hc_sg", [P, C], U8)
+        hc_sg = [
+            sb("hc_sg0", [P, HALF], U8),
+            shared.tile([P, HALF], U8, name="hc_sg1", align_bytes=64, offset=9 * C),
+        ]
         hc_sd = sb("hc_sd", [P, C], U8)
         hc_wg = shared.tile([P, C], U32, name="hc_wg", align_bytes=64, offset=0)
         hc_w = sb("hc_w", [P, C], U32)
-        ca_w = shared.tile([P, C], U32, name="ca_w", align_bytes=64, offset=4 * C)
-        ca_s = keep.tile([P, C], U8, name="ca_s", tag="w1w_then_ca_s", align_bytes=64)
+        ca_wg = shared.tile([P, C], U32, name="ca_wg", align_bytes=64, offset=4 * C)
+        ca_w = sb("ca_w", [P, C], U32)
+        ca_sg = shared.tile([P, C], U8, name="ca_sg", align_bytes=64, offset=8 * C)
+        ca_s = sb("ca_s", [P, C], U8)
 
         nc.vector.tensor_copy(xq_s[:], xs[:].indirect(lists["offs"][:]))
-        nc.vector.tensor_copy(hc_sg[:], xs[:].indirect(lists["hc"][:]))
+        nc.vector.tensor_copy(hc_sg[0][:], xs[:].indirect(half_list("hc", 0)))
         nc.vector.tensor_copy(xq_w[:], xw[:].indirect(lists["offs"][:]))
         nc.vector.tensor_copy(dealt(w1s_d[:], 16), undealt(w1s[:], 16))
 
@@ -110,16 +115,20 @@ def tile_picked_cdhgatebrange_none_po_kernel(
                 stop=True,
             )
 
-        nc.vector.tensor_copy(dealt(hc_sd[:], 16), undealt(hc_sg[:], 16))
+        nc.vector.tensor_copy(hc_sg[1][:], xs[:].indirect(half_list("hc", 1)))
+        nc.vector.tensor_copy(hc_wg[:], xw[:].indirect(lists["hc"][:]))
+        for h in range(2):
+            nc.vector.tensor_copy(dealt(hc_sd[:], 16)[:, 4 * h : 4 * h + 4], undealt(hc_sg[h][:], 16))
         hc_sd32 = hc_sd[:].bitcast(I32)
         hc_s32 = hc_s[:].bitcast(I32)
         for r in range(4):
             src = 16 * (r // 2) + r
             nc.sync.dma_start(hc_s32[r:P:32, :], hc_sd32[src:P:32, :])
-        nc.vector.tensor_copy(hc_wg[:], xw[:].indirect(lists["hc"][:]))
-        nc.vector.tensor_copy(ca_w[:].rearrange("p (t m) -> p m t", t=PACK), xw[:].indirect(lists["ca"][:]))
+        nc.vector.tensor_copy(ca_wg[:], xw[:].indirect(lists["ca"][:]))
         nc.vector.tensor_copy(dealt(hc_w[:], 4), undealt(hc_wg[:], 4))
-        nc.vector.tensor_copy(ca_s[:].rearrange("p (t m) -> p m t", t=PACK), xs[:].indirect(lists["ca"][:]))
+        nc.vector.tensor_copy(ca_sg[:], xs[:].indirect(lists["ca"][:]))
+        nc.vector.tensor_copy(dealt(ca_w[:], 4), undealt(ca_wg[:], 4))
+        nc.vector.tensor_copy(dealt(ca_s[:], 16), undealt(ca_sg[:], 16))
 
         def halves(name, dtype):
             return [sb(f"{name}{h}", [P, PACK, HALF], dtype) for h in range(2)]
@@ -128,7 +137,7 @@ def tile_picked_cdhgatebrange_none_po_kernel(
         top2, low2 = halves("top2", F32), halves("low2", F32)
         top3, low3 = halves("top3", F32), halves("low3", F32)
         spread = halves("spread", F32)
-        z_rows = sb("z_rows", [P, PACK, HALF], BF16)
+        z_rows = halves("z_rows", BF16)
         z_bf = [sb(f"z_bf{h}", [P, HALF * PACK], BF16) for h in range(2)]
         z_w = [sb(f"z_w{h}", [P, HALF], U32) for h in range(2)]
         z_s = [sb(f"z_s{h}", [P, HALF], U8) for h in range(2)]
@@ -145,15 +154,16 @@ def tile_picked_cdhgatebrange_none_po_kernel(
             nc.vector.scalar_tensor_tensor(
                 spread[h][:, t, :], low3[h][:, t, :], -0.5, top3[h][:, t, :], ALU.mult, ALU.add
             )
-            if h == 0:
-                nc.scalar.activation(z_rows[:, t, :], spread[h][:, t, :], ACT.Copy, scale=g[:, t : t + 1])
+            if (h, t) == (1, PACK - 1):
+                nc.vector.tensor_scalar(z_rows[h][:, t, :], spread[h][:, t, :], g[:, t : t + 1], None, ALU.mult)
+            else:
+                nc.scalar.activation(z_rows[h][:, t, :], spread[h][:, t, :], ACT.Copy, scale=g[:, t : t + 1])
 
         def weave_z(h):
             if h == 0:
-                nc.scalar.copy(woven_view(z_bf[h]), rows_view(z_rows))
+                nc.scalar.copy(woven_view(z_bf[h]), rows_view(z_rows[h]))
             else:
-                g_view = g[:].unsqueeze(1).unsqueeze(3).to_broadcast([P, HALF // 4, PACK, 4])
-                nc.vector.tensor_tensor(woven_view(z_bf[h]), rows_view(spread[h]), g_view, ALU.mult)
+                nc.vector.tensor_copy(woven_view(z_bf[h]), rows_view(z_rows[h]))
 
         def score_psum(h, t, side):
             if h == 0:
@@ -215,15 +225,19 @@ def tile_picked_cdhgatebrange_none_po_kernel(
         gate, gated, res = halves("gate", F32), halves("gated", F32), halves("res", F32)
         res_bf = [sb(f"res_bf{h}", [P, HALF * PACK], BF16) for h in range(2)]
         res_w = [sb(f"res_w{h}", [P, HALF], U32) for h in range(2)]
+        picked = sb("picked", [P, PACK - 1, HALF], F32)
         res_s = sb("res_s", [P, S], U8)
         out_rows = out_0.rearrange("(p t) j -> p t j", t=PACK)
         out_words = out_1[0].rearrange("p n t -> p (n t)").bitcast(I32)
 
         def finish(h, t):
             js = slice(h * HALF, (h + 1) * HALF)
-            nc.vector.tensor_tensor(
-                res[h][:, t, :], na[t][:].indirect(half_list("n3", h)), gated[h][:, t, :], ALU.subtract
-            )
+            if h == 1 and t > 0:
+                nc.vector.tensor_tensor(res[h][:, t, :], picked[:, t - 1, :], gated[h][:, t, :], ALU.subtract)
+            else:
+                nc.vector.tensor_tensor(
+                    res[h][:, t, :], na[t][:].indirect(half_list("n3", h)), gated[h][:, t, :], ALU.subtract
+                )
             nc.sync.dma_start(out_rows[:, t, js], res[h][:, t, :])
 
         def planes(h):
@@ -236,13 +250,15 @@ def tile_picked_cdhgatebrange_none_po_kernel(
             if h == 0:
                 empty_b(1, t)
             nc.scalar.activation(gate[h][:, t, :], th[t][:].indirect(half_list("n4", h)), ACT.Copy)
+            if h == 1 and t > 0:
+                nc.scalar.activation(picked[:, t - 1, :], na[t][:].indirect(half_list("n3", h)), ACT.Copy)
             nc.vector.scalar_tensor_tensor(gated[h][:, t, :], gate[h][:, t, :], 1.0, na[t][:, js], ALU.add, ALU.mult)
             if u > 0:
                 finish(*units[u - 1])
         nc.scalar.copy(woven_view(res_bf[0]), rows_view(res[0]))
         finish(*units[-1])
-        planes(0)
         nc.vector.tensor_copy(woven_view(res_bf[1]), rows_view(res[1]))
+        planes(0)
         planes(1)
         res_s32 = res_s[:].bitcast(I32)
         out_scales = out_2[0].bitcast(I32)

@@ -99,7 +99,8 @@ def tile_picked_cdhgatebrange_none_po_kernel(
         nc.vector.tensor_copy(xq_s[:], xs[:].indirect(lists["offs"][:]))
         nc.vector.tensor_copy(hc_sg[0][:], xs[:].indirect(half_list("hc", 0)))
         nc.vector.tensor_copy(xq_w[:], xw[:].indirect(lists["offs"][:]))
-        nc.vector.tensor_copy(dealt(w1s_d[:], 16), undealt(w1s[:], 16))
+        for ts in (slice(0, 1), slice(1, PACK)):
+            nc.vector.tensor_copy(dealt(w1s_d[:], 16)[:, :, ts], undealt(w1s[:], 16)[:, :, ts])
 
         banks = [psum.tile([P, S], F32, name=f"bank{b}") for b in range(8)]
         y = [sb(f"y{t}", [P, S], F32) for t in range(PACK)]
@@ -133,10 +134,10 @@ def tile_picked_cdhgatebrange_none_po_kernel(
         def halves(name, dtype):
             return [sb(f"{name}{h}", [P, PACK, HALF], dtype) for h in range(2)]
 
-        pa, pb = halves("pa", F32), halves("pb", F32)
+        pab = [sb(f"pab{u}", [P, 2, HALF], F32) for u in range(2 * PACK)]
         top2, low2 = halves("top2", F32), halves("low2", F32)
         top3, low3 = halves("top3", F32), halves("low3", F32)
-        spread = halves("spread", F32)
+        spread = sb("spread", [P, 2, HALF], F32)
         z_rows = halves("z_rows", BF16)
         z_bf = [sb(f"z_bf{h}", [P, HALF * PACK], BF16) for h in range(2)]
         z_w = [sb(f"z_w{h}", [P, HALF], U32) for h in range(2)]
@@ -150,14 +151,8 @@ def tile_picked_cdhgatebrange_none_po_kernel(
         def woven_view(tile):
             return tile[:].rearrange("p (c i t) -> p c t i", t=PACK, i=4)
 
-        def combine(h, t):
-            nc.vector.scalar_tensor_tensor(
-                spread[h][:, t, :], low3[h][:, t, :], -0.5, top3[h][:, t, :], ALU.mult, ALU.add
-            )
-            if (h, t) == (1, PACK - 1):
-                nc.vector.tensor_scalar(z_rows[h][:, t, :], spread[h][:, t, :], g[:, t : t + 1], None, ALU.mult)
-            else:
-                nc.scalar.activation(z_rows[h][:, t, :], spread[h][:, t, :], ACT.Copy, scale=g[:, t : t + 1])
+        def scale_z(h, t, src):
+            nc.scalar.activation(z_rows[h][:, t, :], src, ACT.Copy, scale=g[:, t : t + 1])
 
         def weave_z(h):
             if h == 0:
@@ -168,13 +163,15 @@ def tile_picked_cdhgatebrange_none_po_kernel(
         def score_psum(h, t, side):
             if h == 0:
                 return banks[PACK + t][:, side * HALF : (side + 1) * HALF]
-            return banks[PACK * side + t][:, 0:HALF]
+            return banks[2 * side + t // 2][:, (t % 2) * HALF : (t % 2 + 1) * HALF]
 
         def score(h):
             nc.vector.quantize_mx(out=z_w[h][:].bitcast(FP8X4), scales=z_s[h][:], in_=z_bf[h][:])
-            for t in range(PACK):
-                cols = slice(t * P, (t + 1) * P)
-                for side, (words, scales) in enumerate(((hc_w, hc_s), (ca_w, ca_s))):
+            operands = ((hc_w, hc_s), (ca_w, ca_s))
+            for t0, side in [(t0, side) for t0 in (0, 2) for side in range(2)]:
+                words, scales = operands[side]
+                for t in (t0, t0 + 1):
+                    cols = slice(t * P, (t + 1) * P)
                     nc.tensor.matmul_mx(
                         out=score_psum(h, t, side),
                         lhsT=words[:, cols].bitcast(FP8X4),
@@ -197,23 +194,43 @@ def tile_picked_cdhgatebrange_none_po_kernel(
                 nc.vector.tensor_scalar(na[t][:, js], score_psum(h, t, 1), -0.0625 * 0.5, None, ALU.mult)
 
         units = [(h, t) for h in range(2) for t in range(PACK)]
-        for u, (h, t) in enumerate(units):
+        for pair in range(PACK):
+            h, t0 = pair // 2, 2 * (pair % 2)
             js = slice(h * HALF, (h + 1) * HALF)
-            if h == 0:
-                nc.scalar.activation(y[t][:], banks[t][:], ACT.Copy)
-            nc.scalar.activation(pa[h][:, t, :], y[t][:].indirect(half_list("n1", h)), ACT.Copy)
-            nc.scalar.activation(pb[h][:, t, :], y[t][:].indirect(half_list("n2", h)), ACT.Copy)
-            nc.vector.tensor_tensor(top2[h][:, t, :], pa[h][:, t, :], pb[h][:, t, :], ALU.max)
-            nc.vector.tensor_tensor(low2[h][:, t, :], pa[h][:, t, :], pb[h][:, t, :], ALU.min)
-            if u > 0:
-                combine(*units[u - 1])
-            nc.vector.tensor_tensor(top3[h][:, t, :], top2[h][:, t, :], y[t][:, js], ALU.max)
-            nc.vector.tensor_tensor(low3[h][:, t, :], low2[h][:, t, :], y[t][:, js], ALU.min)
-            if (h, t) == (1, 2):
-                weave_z(0)
-            if (h, t) == (1, 3):
+            for t in (t0, t0 + 1):
+                both = pab[PACK * h + t]
+                if h == 0:
+                    nc.scalar.activation(y[t][:], banks[t][:], ACT.Copy)
+                nc.scalar.activation(both[:, 0, :], y[t][:].indirect(half_list("n1", h)), ACT.Copy)
+                nc.scalar.activation(both[:, 1, :], y[t][:].indirect(half_list("n2", h)), ACT.Copy, scale=0.5)
+            for t in (t0, t0 + 1):
+                both = pab[PACK * h + t]
+                nc.vector.scalar_tensor_tensor(top2[h][:, t, :], both[:, 1, :], 2.0, both[:, 0, :], ALU.mult, ALU.max)
+            for t in (t0, t0 + 1):
+                both = pab[PACK * h + t]
+                nc.vector.scalar_tensor_tensor(low2[h][:, t, :], both[:, 0, :], 0.5, both[:, 1, :], ALU.mult, ALU.min)
+            if pair > 0:
+                ph, pt = (pair - 1) // 2, 2 * ((pair - 1) % 2)
+                freed = pab[PACK * h + t0]
+                nc.gpsimd.tensor_tensor(
+                    freed[:], top3[ph][:, pt : pt + 2, :], low3[ph][:, pt : pt + 2, :], ALU.subtract
+                )
+                for i in range(2):
+                    scale_z(ph, pt + i, freed[:, i, :])
+            for t in (t0, t0 + 1):
+                nc.vector.tensor_tensor(top3[h][:, t, :], top2[h][:, t, :], banks[t][:, js], ALU.max)
+            if pair == 3:
                 score(0)
-        combine(*units[-1])
+            for t in (t0, t0 + 1):
+                nc.vector.scalar_tensor_tensor(
+                    low3[h][:, t, :], banks[t][:, js], 0.5, low2[h][:, t, :], ALU.mult, ALU.min
+                )
+            if pair == 2:
+                weave_z(0)
+        for i in range(2):
+            nc.vector.tensor_tensor(spread[:, i, :], top3[1][:, 2 + i, :], low3[1][:, 2 + i, :], ALU.subtract)
+        for i in range(2):
+            nc.vector.tensor_scalar(z_rows[1][:, 2 + i, :], spread[:, i, :], g[:, 2 + i : 3 + i], None, ALU.mult)
         for t in range(PACK):
             empty_b(0, t)
             empty_a(0, t)
@@ -225,15 +242,15 @@ def tile_picked_cdhgatebrange_none_po_kernel(
         gate, gated, res = halves("gate", F32), halves("gated", F32), halves("res", F32)
         res_bf = [sb(f"res_bf{h}", [P, HALF * PACK], BF16) for h in range(2)]
         res_w = [sb(f"res_w{h}", [P, HALF], U32) for h in range(2)]
-        picked = sb("picked", [P, PACK - 1, HALF], F32)
+        picked = sb("picked", [P, 2, HALF], F32)
         res_s = sb("res_s", [P, S], U8)
         out_rows = out_0.rearrange("(p t) j -> p t j", t=PACK)
         out_words = out_1[0].rearrange("p n t -> p (n t)").bitcast(I32)
 
         def finish(h, t):
             js = slice(h * HALF, (h + 1) * HALF)
-            if h == 1 and t > 0:
-                nc.vector.tensor_tensor(res[h][:, t, :], picked[:, t - 1, :], gated[h][:, t, :], ALU.subtract)
+            if h == 1 and t > 1:
+                nc.vector.tensor_tensor(res[h][:, t, :], picked[:, t - 2, :], gated[h][:, t, :], ALU.subtract)
             else:
                 nc.vector.tensor_tensor(
                     res[h][:, t, :], na[t][:].indirect(half_list("n3", h)), gated[h][:, t, :], ALU.subtract
@@ -250,8 +267,8 @@ def tile_picked_cdhgatebrange_none_po_kernel(
             if h == 0:
                 empty_b(1, t)
             nc.scalar.activation(gate[h][:, t, :], th[t][:].indirect(half_list("n4", h)), ACT.Copy)
-            if h == 1 and t > 0:
-                nc.scalar.activation(picked[:, t - 1, :], na[t][:].indirect(half_list("n3", h)), ACT.Copy)
+            if h == 1 and t > 1:
+                nc.scalar.activation(picked[:, t - 2, :], na[t][:].indirect(half_list("n3", h)), ACT.Copy)
             nc.vector.scalar_tensor_tensor(gated[h][:, t, :], gate[h][:, t, :], 1.0, na[t][:, js], ALU.add, ALU.mult)
             if u > 0:
                 finish(*units[u - 1])

@@ -91,10 +91,8 @@ def tile_picked_cdhgatebrange_none_po_kernel(
         hc_sd = sb("hc_sd", [P, C], U8)
         hc_wg = shared.tile([P, C], U32, name="hc_wg", align_bytes=64, offset=0)
         hc_w = sb("hc_w", [P, C], U32)
-        ca_wg = shared.tile([P, C], U32, name="ca_wg", align_bytes=64, offset=4 * C)
-        ca_w = sb("ca_w", [P, C], U32)
-        ca_sg = shared.tile([P, C], U8, name="ca_sg", align_bytes=64, offset=8 * C)
-        ca_s = sb("ca_s", [P, C], U8)
+        ca_w = shared.tile([P, C], U32, name="ca_w", align_bytes=64, offset=4 * C)
+        ca_s = shared.tile([P, C], U8, name="ca_s", align_bytes=64, offset=8 * C)
 
         nc.vector.tensor_copy(xq_s[:], xs[:].indirect(lists["offs"][:]))
         nc.vector.tensor_copy(hc_sg[0][:], xs[:].indirect(half_list("hc", 0)))
@@ -125,20 +123,20 @@ def tile_picked_cdhgatebrange_none_po_kernel(
         for r in range(4):
             src = 16 * (r // 2) + r
             nc.sync.dma_start(hc_s32[r:P:32, :], hc_sd32[src:P:32, :])
-        nc.vector.tensor_copy(ca_wg[:], xw[:].indirect(lists["ca"][:]))
+        nc.vector.tensor_copy(ca_w[:].rearrange("p (t m) -> p m t", t=PACK), xw[:].indirect(lists["ca"][:]))
         nc.vector.tensor_copy(dealt(hc_w[:], 4), undealt(hc_wg[:], 4))
-        nc.vector.tensor_copy(ca_sg[:], xs[:].indirect(lists["ca"][:]))
-        nc.vector.tensor_copy(dealt(ca_w[:], 4), undealt(ca_wg[:], 4))
-        nc.vector.tensor_copy(dealt(ca_s[:], 16), undealt(ca_sg[:], 16))
+        nc.vector.tensor_copy(ca_s[:].rearrange("p (t m) -> p m t", t=PACK), xs[:].indirect(lists["ca"][:]))
 
         def halves(name, dtype):
             return [sb(f"{name}{h}", [P, PACK, HALF], dtype) for h in range(2)]
 
-        pab = [sb(f"pab{u}", [P, 2, HALF], F32) for u in range(2 * PACK)]
+        spread = sb("spread", [P, PACK, HALF], F32)
+        pab = [
+            spread[:, 0:2, :] if u == 6 else sb(f"pab{u}", [P, 2, HALF], F32)[:] for u in range(2 * PACK)
+        ]
         top2, low2 = halves("top2", F32), halves("low2", F32)
         top3, low3 = halves("top3", F32), halves("low3", F32)
-        spread = sb("spread", [P, 2, HALF], F32)
-        z_rows = halves("z_rows", BF16)
+        z_rows = sb("z_rows", [P, PACK, HALF], BF16)
         z_bf = [sb(f"z_bf{h}", [P, HALF * PACK], BF16) for h in range(2)]
         z_w = [sb(f"z_w{h}", [P, HALF], U32) for h in range(2)]
         z_s = [sb(f"z_s{h}", [P, HALF], U8) for h in range(2)]
@@ -152,26 +150,26 @@ def tile_picked_cdhgatebrange_none_po_kernel(
             return tile[:].rearrange("p (c i t) -> p c t i", t=PACK, i=4)
 
         def scale_z(h, t, src):
-            nc.scalar.activation(z_rows[h][:, t, :], src, ACT.Copy, scale=g[:, t : t + 1])
+            nc.scalar.activation(z_rows[:, t, :], src, ACT.Copy, scale=g[:, t : t + 1])
 
         def weave_z(h):
             if h == 0:
-                nc.scalar.copy(woven_view(z_bf[h]), rows_view(z_rows[h]))
+                nc.scalar.copy(woven_view(z_bf[h]), rows_view(z_rows))
             else:
-                nc.vector.tensor_copy(woven_view(z_bf[h]), rows_view(z_rows[h]))
+                g_view = g[:].unsqueeze(1).unsqueeze(3).to_broadcast([P, HALF // 4, PACK, 4])
+                nc.vector.tensor_tensor(woven_view(z_bf[h]), rows_view(spread), g_view, ALU.mult)
 
         def score_psum(h, t, side):
             if h == 0:
                 return banks[PACK + t][:, side * HALF : (side + 1) * HALF]
-            return banks[2 * side + t // 2][:, (t % 2) * HALF : (t % 2 + 1) * HALF]
+            return banks[PACK * side + t][:, 0:HALF]
 
         def score(h):
             nc.vector.quantize_mx(out=z_w[h][:].bitcast(FP8X4), scales=z_s[h][:], in_=z_bf[h][:])
             operands = ((hc_w, hc_s), (ca_w, ca_s))
-            for t0, side in [(t0, side) for t0 in (0, 2) for side in range(2)]:
-                words, scales = operands[side]
-                for t in (t0, t0 + 1):
-                    cols = slice(t * P, (t + 1) * P)
+            for t in range(PACK):
+                cols = slice(t * P, (t + 1) * P)
+                for side, (words, scales) in enumerate(operands):
                     nc.tensor.matmul_mx(
                         out=score_psum(h, t, side),
                         lhsT=words[:, cols].bitcast(FP8X4),
@@ -201,7 +199,10 @@ def tile_picked_cdhgatebrange_none_po_kernel(
                 both = pab[PACK * h + t]
                 if h == 0:
                     nc.scalar.activation(y[t][:], banks[t][:], ACT.Copy)
-                nc.scalar.activation(both[:, 0, :], y[t][:].indirect(half_list("n1", h)), ACT.Copy)
+                if (h, t) == (0, 2):
+                    nc.vector.tensor_copy(both[:, 0, :], y[t][:].indirect(half_list("n1", h)))
+                else:
+                    nc.scalar.activation(both[:, 0, :], y[t][:].indirect(half_list("n1", h)), ACT.Copy)
                 nc.scalar.activation(both[:, 1, :], y[t][:].indirect(half_list("n2", h)), ACT.Copy, scale=0.5)
             for t in (t0, t0 + 1):
                 both = pab[PACK * h + t]
@@ -213,10 +214,11 @@ def tile_picked_cdhgatebrange_none_po_kernel(
                 ph, pt = (pair - 1) // 2, 2 * ((pair - 1) % 2)
                 freed = pab[PACK * h + t0]
                 nc.gpsimd.tensor_tensor(
-                    freed[:], top3[ph][:, pt : pt + 2, :], low3[ph][:, pt : pt + 2, :], ALU.subtract
+                    freed, top3[ph][:, pt : pt + 2, :], low3[ph][:, pt : pt + 2, :], ALU.subtract
                 )
-                for i in range(2):
-                    scale_z(ph, pt + i, freed[:, i, :])
+                if ph == 0:
+                    for i in range(2):
+                        scale_z(ph, pt + i, freed[:, i, :])
             for t in (t0, t0 + 1):
                 nc.vector.tensor_tensor(top3[h][:, t, :], top2[h][:, t, :], banks[t][:, js], ALU.max)
             if pair == 3:
@@ -228,9 +230,7 @@ def tile_picked_cdhgatebrange_none_po_kernel(
             if pair == 2:
                 weave_z(0)
         for i in range(2):
-            nc.vector.tensor_tensor(spread[:, i, :], top3[1][:, 2 + i, :], low3[1][:, 2 + i, :], ALU.subtract)
-        for i in range(2):
-            nc.vector.tensor_scalar(z_rows[1][:, 2 + i, :], spread[:, i, :], g[:, 2 + i : 3 + i], None, ALU.mult)
+            nc.vector.tensor_tensor(spread[:, 2 + i, :], top3[1][:, 2 + i, :], low3[1][:, 2 + i, :], ALU.subtract)
         for t in range(PACK):
             empty_b(0, t)
             empty_a(0, t)
@@ -242,15 +242,15 @@ def tile_picked_cdhgatebrange_none_po_kernel(
         gate, gated, res = halves("gate", F32), halves("gated", F32), halves("res", F32)
         res_bf = [sb(f"res_bf{h}", [P, HALF * PACK], BF16) for h in range(2)]
         res_w = [sb(f"res_w{h}", [P, HALF], U32) for h in range(2)]
-        picked = sb("picked", [P, 2, HALF], F32)
+        picked = sb("picked", [P, HALF], F32)
         res_s = sb("res_s", [P, S], U8)
         out_rows = out_0.rearrange("(p t) j -> p t j", t=PACK)
         out_words = out_1[0].rearrange("p n t -> p (n t)").bitcast(I32)
 
         def finish(h, t):
             js = slice(h * HALF, (h + 1) * HALF)
-            if h == 1 and t > 1:
-                nc.vector.tensor_tensor(res[h][:, t, :], picked[:, t - 2, :], gated[h][:, t, :], ALU.subtract)
+            if (h, t) == units[-1]:
+                nc.vector.tensor_tensor(res[h][:, t, :], picked[:], gated[h][:, t, :], ALU.subtract)
             else:
                 nc.vector.tensor_tensor(
                     res[h][:, t, :], na[t][:].indirect(half_list("n3", h)), gated[h][:, t, :], ALU.subtract
@@ -267,14 +267,15 @@ def tile_picked_cdhgatebrange_none_po_kernel(
             if h == 0:
                 empty_b(1, t)
             nc.scalar.activation(gate[h][:, t, :], th[t][:].indirect(half_list("n4", h)), ACT.Copy)
-            if h == 1 and t > 1:
-                nc.scalar.activation(picked[:, t - 2, :], na[t][:].indirect(half_list("n3", h)), ACT.Copy)
+            if (h, t) == units[-1]:
+                nc.scalar.activation(picked[:], na[t][:].indirect(half_list("n3", h)), ACT.Copy)
             nc.vector.scalar_tensor_tensor(gated[h][:, t, :], gate[h][:, t, :], 1.0, na[t][:, js], ALU.add, ALU.mult)
             if u > 0:
                 finish(*units[u - 1])
         nc.scalar.copy(woven_view(res_bf[0]), rows_view(res[0]))
         finish(*units[-1])
-        nc.vector.tensor_copy(woven_view(res_bf[1]), rows_view(res[1]))
+        nc.scalar.copy(woven_view(res_bf[1])[:, 0:24], rows_view(res[1])[:, 0:24])
+        nc.vector.tensor_copy(woven_view(res_bf[1])[:, 24:], rows_view(res[1])[:, 24:])
         planes(0)
         planes(1)
         res_s32 = res_s[:].bitcast(I32)

from contextlib import ExitStack

import concourse.mybir as mybir

K, T, S, H, C = 512, 2048, 512, 512, 512
FLOPS = 2 * K * H * S + 2 * 2 * K * C * S

F32 = mybir.dt.float32
BF16 = mybir.dt.bfloat16
I32 = mybir.dt.int32
U32 = mybir.dt.uint32
U16 = mybir.dt.uint16
U8 = mybir.dt.uint8
FP8X4 = mybir.dt.float8_e4m3fn_x4
ACT = mybir.ActivationFunctionType
ALU = mybir.AluOpType

P = 128
PACK = 4
HALF = S // 2
LIST_COLS = HALF // 16


def dealt(ap, run):
    return ap.rearrange("p (t c i) -> p c t i", t=PACK, i=run)


def undealt(ap, run):
    return ap.rearrange("p (c i t) -> p c t i", t=PACK, i=run)


def tile_picked_cdhgatebrange_none_po_kernel(
    tc, x_words, x_scales, w1_words, w1_scales, gs, offs, n1, n2, ca, hc, n3, n4, out_0, out_1, out_2
):
    nc = tc.nc
    with ExitStack() as ctx:
        keep = ctx.enter_context(tc.tile_pool(name="keep", bufs=1))
        shared = ctx.enter_context(tc.tile_pool(name="shared", bufs=1))
        psum = ctx.enter_context(tc.psum_pool(name="psum", bufs=1))

        def sb(name, shape, dtype):
            return keep.tile(shape, dtype, name=name, align_bytes=64)

        lists = {}

        def load_list(name, src):
            lists[name] = sb("list_" + name, [P, S // 16], U16)
            nc.sync.dma_start(lists[name][:], src)

        def half_list(name, h):
            return lists[name][:, h * LIST_COLS : (h + 1) * LIST_COLS]

        xw = sb("xw", [P, T], U32)
        xs = sb("xs", [P, T], U8)
        w1w = shared.tile([P, H], U32, name="w1w", align_bytes=64, offset=8 * C)
        w1s = shared.tile([P, H], U8, name="w1s", align_bytes=64, offset=4 * C - H // 2)
        hc_s = sb("hc_s", [P, C], U8)
        g = sb("g", [P, PACK], F32)

        xs32 = xs[:].bitcast(I32)
        w1s32 = w1s[:].bitcast(I32)
        nc.gpsimd.memset(hc_s[:].bitcast(I32), 0)

        xs_hbm = x_scales[0].bitcast(I32)
        w1s_hbm = w1_scales[0].bitcast(I32)
        load_list("offs", offs)
        for q in range(4):
            nc.sync.dma_start(xs32[32 * q : 32 * q + 32, :], xs_hbm[4 * q : 4 * q + 4, :].partition_broadcast(8))
        load_list("hc", hc)
        nc.sync.dma_start(xw[:].bitcast(I32), x_words[0].rearrange("p n t -> p (n t)").bitcast(I32))
        nc.sync.dma_start(w1w[:].bitcast(I32), w1_words[0].rearrange("p n t -> p (n t)").bitcast(I32))
        for q in range(4):
            nc.sync.dma_start(w1s32[32 * q : 32 * q + 32, :], w1s_hbm[4 * q : 4 * q + 4, :].partition_broadcast(8))
        load_list("n1", n1)
        load_list("n2", n2)
        load_list("ca", ca)
        nc.sync.dma_start(g[:], gs.rearrange("(p t) o -> p (t o)", t=PACK))
        load_list("n4", n4)
        load_list("n3", n3)

        w1w_d = sb("w1w_d", [P, H], U32)
        w1s_d = sb("w1s_d", [P, H], U8)
        nc.scalar.copy(dealt(w1w_d[:], 4), undealt(w1w[:], 4))

        xq_w = sb("xq_w", [P, S], U32)
        xq_s = sb("xq_s", [P, S], U8)
        hc_sg = [
            sb("hc_sg0", [P, HALF], U8),
            shared.tile([P, HALF], U8, name="hc_sg1", align_bytes=64, offset=9 * C),
        ]
        hc_sd = sb("hc_sd", [P, C], U8)
        hc_wg = shared.tile([P, C], U32, name="hc_wg", align_bytes=64, offset=0)
        hc_w = sb("hc_w", [P, C], U32)
        ca_w = shared.tile([P, C], U32, name="ca_w", align_bytes=64, offset=4 * C)
        ca_s = shared.tile([P, C], U8, name="ca_s", align_bytes=64, offset=8 * C)

        nc.vector.tensor_copy(xq_s[:], xs[:].indirect(lists["offs"][:]))
        nc.vector.tensor_copy(hc_sg[0][:], xs[:].indirect(half_list("hc", 0)))
        nc.vector.tensor_copy(xq_w[:], xw[:].indirect(lists["offs"][:]))
        for ts in (slice(0, 1), slice(1, PACK)):
            nc.vector.tensor_copy(dealt(w1s_d[:], 16)[:, :, ts], undealt(w1s[:], 16)[:, :, ts])

        banks = [psum.tile([P, S], F32, name=f"bank{b}") for b in range(8)]
        y = [sb(f"y{t}", [P, S], F32) for t in range(PACK)]
        for t in range(PACK):
            cols = slice(t * P, (t + 1) * P)
            nc.tensor.matmul_mx(
                out=banks[t][:],
                lhsT=w1w_d[:, cols].bitcast(FP8X4),
                lhsT_scale=w1s_d[:, cols],
                rhs=xq_w[:].bitcast(FP8X4),
                rhs_scale=xq_s[:],
                start=True,
                stop=True,
            )

        nc.vector.tensor_copy(hc_sg[1][:], xs[:].indirect(half_list("hc", 1)))
        nc.vector.tensor_copy(hc_wg[:], xw[:].indirect(lists["hc"][:]))
        for h in range(2):
            nc.vector.tensor_copy(dealt(hc_sd[:], 16)[:, 4 * h : 4 * h + 4], undealt(hc_sg[h][:], 16))
        hc_sd32 = hc_sd[:].bitcast(I32)
        hc_s32 = hc_s[:].bitcast(I32)
        for r in range(4):
            src = 16 * (r // 2) + r
            nc.sync.dma_start(hc_s32[r:P:32, :], hc_sd32[src:P:32, :])
        nc.vector.tensor_copy(ca_w[:].rearrange("p (t m) -> p m t", t=PACK), xw[:].indirect(lists["ca"][:]))
        nc.vector.tensor_copy(dealt(hc_w[:], 4), undealt(hc_wg[:], 4))
        nc.vector.tensor_copy(ca_s[:].rearrange("p (t m) -> p m t", t=PACK), xs[:].indirect(lists["ca"][:]))

        def halves(name, dtype):
            return [sb(f"{name}{h}", [P, PACK, HALF], dtype) for h in range(2)]

        spread = sb("spread", [P, PACK, HALF], F32)
        pab = [
            spread[:, 0:2, :] if u == 6 else sb(f"pab{u}", [P, 2, HALF], F32)[:] for u in range(2 * PACK)
        ]
        top2, low2 = halves("top2", F32), halves("low2", F32)
        top3, low3 = halves("top3", F32), halves("low3", F32)
        z_rows = sb("z_rows", [P, PACK, HALF], BF16)
        z_bf = [sb(f"z_bf{h}", [P, HALF * PACK], BF16) for h in range(2)]
        z_w = [sb(f"z_w{h}", [P, HALF], U32) for h in range(2)]
        z_s = [sb(f"z_s{h}", [P, HALF], U8) for h in range(2)]
        na = [sb(f"na{t}", [P, S], F32) for t in range(PACK)]
        th = [sb(f"th{t}", [P, S], F32) for t in range(PACK)]

        def rows_view(tile):
            return tile[:].rearrange("p t (c i) -> p c t i", i=4)

        def woven_view(tile):
            return tile[:].rearrange("p (c i t) -> p c t i", t=PACK, i=4)

        def scale_z(h, t, src):
            nc.scalar.activation(z_rows[:, t, :], src, ACT.Copy, scale=g[:, t : t + 1])

        def weave_z(h):
            if h == 0:
                nc.scalar.copy(woven_view(z_bf[h]), rows_view(z_rows))
            else:
                g_view = g[:].unsqueeze(1).unsqueeze(3).to_broadcast([P, HALF // 4, PACK, 4])
                nc.vector.tensor_tensor(woven_view(z_bf[h]), rows_view(spread), g_view, ALU.mult)

        def score_psum(h, t, side):
            if h == 0:
                return banks[PACK + t][:, side * HALF : (side + 1) * HALF]
            return banks[PACK * side + t][:, 0:HALF]

        def score(h):
            nc.vector.quantize_mx(out=z_w[h][:].bitcast(FP8X4), scales=z_s[h][:], in_=z_bf[h][:])
            operands = ((hc_w, hc_s), (ca_w, ca_s))
            for t in range(PACK):
                cols = slice(t * P, (t + 1) * P)
                for side, (words, scales) in enumerate(operands):
                    nc.tensor.matmul_mx(
                        out=score_psum(h, t, side),
                        lhsT=words[:, cols].bitcast(FP8X4),
                        lhsT_scale=scales[:, cols],
                        rhs=z_w[h][:].bitcast(FP8X4),
                        rhs_scale=z_s[h][:],
                        start=True,
                        stop=True,
                    )

        def empty_b(h, t):
            js = slice(h * HALF, (h + 1) * HALF)
            nc.scalar.activation(th[t][:, js], score_psum(h, t, 0), ACT.Tanh, scale=0.0625 * 0.5)

        def empty_a(h, t):
            js = slice(h * HALF, (h + 1) * HALF)
            if h == 0:
                nc.scalar.activation(na[t][:, js], score_psum(h, t, 1), ACT.Copy, scale=-0.0625 * 0.5)
            else:
                nc.vector.tensor_scalar(na[t][:, js], score_psum(h, t, 1), -0.0625 * 0.5, None, ALU.mult)

        units = [(h, t) for h in range(2) for t in range(PACK)]
        for pair in range(PACK):
            h, t0 = pair // 2, 2 * (pair % 2)
            js = slice(h * HALF, (h + 1) * HALF)
            for t in (t0, t0 + 1):
                both = pab[PACK * h + t]
                if h == 0:
                    nc.scalar.activation(y[t][:], banks[t][:], ACT.Copy)
                if (h, t) == (0, 2):
                    nc.vector.tensor_copy(both[:, 0, :], y[t][:].indirect(half_list("n1", h)))
                else:
                    nc.scalar.activation(both[:, 0, :], y[t][:].indirect(half_list("n1", h)), ACT.Copy)
                nc.scalar.activation(both[:, 1, :], y[t][:].indirect(half_list("n2", h)), ACT.Copy, scale=0.5)
            for t in (t0, t0 + 1):
                both = pab[PACK * h + t]
                nc.vector.scalar_tensor_tensor(top2[h][:, t, :], both[:, 1, :], 2.0, both[:, 0, :], ALU.mult, ALU.max)
            for t in (t0, t0 + 1):
                both = pab[PACK * h + t]
                nc.vector.scalar_tensor_tensor(low2[h][:, t, :], both[:, 0, :], 0.5, both[:, 1, :], ALU.mult, ALU.min)
            if pair > 0:
                ph, pt = (pair - 1) // 2, 2 * ((pair - 1) % 2)
                freed = pab[PACK * h + t0]
                nc.gpsimd.tensor_tensor(
                    freed, top3[ph][:, pt : pt + 2, :], low3[ph][:, pt : pt + 2, :], ALU.subtract
                )
                if ph == 0:
                    for i in range(2):
                        scale_z(ph, pt + i, freed[:, i, :])
            for t in (t0, t0 + 1):
                nc.vector.tensor_tensor(top3[h][:, t, :], top2[h][:, t, :], banks[t][:, js], ALU.max)
            if pair == 3:
                score(0)
            for t in (t0, t0 + 1):
                nc.vector.scalar_tensor_tensor(
                    low3[h][:, t, :], banks[t][:, js], 0.5, low2[h][:, t, :], ALU.mult, ALU.min
                )
            if pair == 2:
                weave_z(0)
        for i in range(2):
            nc.vector.tensor_tensor(spread[:, 2 + i, :], top3[1][:, 2 + i, :], low3[1][:, 2 + i, :], ALU.subtract)
        for t in range(PACK):
            empty_b(0, t)
            empty_a(0, t)
        weave_z(1)
        score(1)
        for t in range(PACK):
            empty_a(1, t)

        gate, gated, res = halves("gate", F32), halves("gated", F32), halves("res", F32)
        res_bf = [sb(f"res_bf{h}", [P, HALF * PACK], BF16) for h in range(2)]
        res_w = [sb(f"res_w{h}", [P, HALF], U32) for h in range(2)]
        picked = sb("picked", [P, HALF], F32)
        res_s = sb("res_s", [P, S], U8)
        out_rows = out_0.rearrange("(p t) j -> p t j", t=PACK)
        out_words = out_1[0].rearrange("p n t -> p (n t)").bitcast(I32)

        def finish(h, t):
            js = slice(h * HALF, (h + 1) * HALF)
            if (h, t) == units[-1]:
                nc.vector.tensor_tensor(res[h][:, t, :], picked[:], gated[h][:, t, :], ALU.subtract)
            else:
                nc.vector.tensor_tensor(
                    res[h][:, t, :], na[t][:].indirect(half_list("n3", h)), gated[h][:, t, :], ALU.subtract
                )
            nc.sync.dma_start(out_rows[:, t, js], res[h][:, t, :])

        def planes(h):
            js = slice(h * HALF, (h + 1) * HALF)
            nc.vector.quantize_mx(out=res_w[h][:].bitcast(FP8X4), scales=res_s[:, js], in_=res_bf[h][:])
            nc.sync.dma_start(out_words[:, js], res_w[h][:].bitcast(I32))

        for u, (h, t) in enumerate(units):
            js = slice(h * HALF, (h + 1) * HALF)
            if h == 0:
                empty_b(1, t)
            nc.scalar.activation(gate[h][:, t, :], th[t][:].indirect(half_list("n4", h)), ACT.Copy)
            if (h, t) == units[-1]:
                nc.scalar.activation(picked[:], na[t][:].indirect(half_list("n3", h)), ACT.Copy)
            nc.vector.scalar_tensor_tensor(gated[h][:, t, :], gate[h][:, t, :], 1.0, na[t][:, js], ALU.add, ALU.mult)
            if u > 0:
                finish(*units[u - 1])
        nc.scalar.copy(woven_view(res_bf[0]), rows_view(res[0]))
        finish(*units[-1])
        nc.scalar.copy(woven_view(res_bf[1])[:, 0:24], rows_view(res[1])[:, 0:24])
        nc.vector.tensor_copy(woven_view(res_bf[1])[:, 24:], rows_view(res[1])[:, 24:])
        planes(0)
        planes(1)
        res_s32 = res_s[:].bitcast(I32)
        out_scales = out_2[0].bitcast(I32)
        for q in range(4):
            queue = nc.sync if q % 2 == 0 else nc.scalar
            queue.dma_start(out_scales[4 * q : 4 * q + 4, :], res_s32[32 * q : 32 * q + 4, :])
